import numpy as np
import ml_dtypes


def mxq(x, axis, fmt="e4m3"):
    dtype, down = {"e4m3": (ml_dtypes.float8_e4m3fn, 7), "e5m2": (ml_dtypes.float8_e5m2, 14)}[fmt]
    v = np.moveaxis(np.asarray(x, np.float32).astype(ml_dtypes.bfloat16).astype(np.float64), axis, -1)
    blocks = v.reshape(v.shape[:-1] + (-1, 32))
    amax = np.abs(blocks).max(-1, keepdims=True)
    byte = np.maximum(np.where(amax > 0, np.frexp(amax)[1] - 1 + 127, 0) - down, 1)
    scale = np.exp2(byte - 127.0)
    codes = (blocks / scale).astype(np.float32).astype(dtype).astype(np.float64)
    return np.moveaxis((codes * scale).reshape(v.shape), -1, axis)


WIDE = False


def mx_kscale(k):
    if not WIDE:
        return np.ones(k)
    levels = np.array([10, -10, 5, -5, 0])
    if k % 512:
        return np.exp2(np.random.permutation(np.resize(levels, k // 32))).repeat(32)
    a = np.empty((k // 512, 16))
    for p in range(k // 512):
        a[p, :8] = np.random.permutation(np.resize(levels, 8))
        for g in range(8):
            far = levels[np.abs(levels - a[p, g]) >= 10]
            a[p, g + 8] = far[np.random.randint(len(far))]
    return np.exp2(a.ravel()).repeat(32)


def f64(x):
    return np.asarray(x).astype(np.float64)


def striped(idx):
    return np.tile(idx.reshape(-1, 16).T, (8, 1)).astype(np.uint16)


def unstriped(offs):
    return offs[:16].T.reshape(-1).astype(np.int64)


def striped8(idx):
    return np.concatenate([x.reshape(-1, 16).T for x in idx]).astype(np.uint16)


def runs(offs, k):
    lists = np.stack([offs[16 * r : 16 * r + 16].T.reshape(-1) for r in range(8)]).astype(np.int64)
    return lists[np.arange(k) % 512 // 64]


def pack_weight(w):
    k, n = w.shape
    w = f64(np.asarray(w, np.float32).astype(ml_dtypes.bfloat16)).reshape(k // 32, 32, n)
    amax = np.abs(w).max(1)
    byte = np.clip(np.where(amax > 0, np.frexp(amax)[1] - 1 + 127 - 7, 1), 1, 254)
    scaled = (w * np.exp2(127.0 - byte)[:, None, :]).reshape(k, n).astype(np.float32)
    words = np.ascontiguousarray(scaled.reshape(k // 512, 128, 4, n).transpose(0, 1, 3, 2)).astype(ml_dtypes.float8_e4m3fn).view(np.uint8)
    return words, np.ascontiguousarray(byte.astype(np.uint8).reshape(k // 512, 16, n))


def unpack_weight(words, scales):
    g, p, n, _ = words.shape
    vals = np.ascontiguousarray(words).view(ml_dtypes.float8_e4m3fn).astype(np.float64) * np.repeat(np.exp2(scales.astype(np.float64) - 127.0), 8, axis=1)[..., None]
    return vals.transpose(0, 1, 3, 2).reshape(g * 512, n)


E2M1 = np.array([0.0, 0.5, 1.0, 1.5, 2.0, 3.0, 4.0, 6.0, -0.0, -0.5, -1.0, -1.5, -2.0, -3.0, -4.0, -6.0])


def pack_fp4(w):
    k, n = w.shape
    w = f64(np.asarray(w, np.float32).astype(ml_dtypes.bfloat16)).reshape(k // 32, 32, n)
    amax = np.abs(w).max(1)
    mant, ex = np.frexp(amax / 6.0)
    byte = np.clip(np.where(amax > 0, np.where(mant > 0.5, ex, ex - 1) + 127, 1), 1, 254)
    scaled = (w * np.exp2(127.0 - byte)[:, None, :]).reshape(k, n).astype(np.float32)
    c = np.ascontiguousarray(scaled.reshape(k // 512, 128, 4, n).transpose(0, 1, 3, 2)).astype(ml_dtypes.float4_e2m1fn).view(np.uint8) & 0xF
    words = (c[..., 0::2] | (c[..., 1::2] << 4)).reshape(k // 512, 128, 2 * n)
    return np.ascontiguousarray(words), np.ascontiguousarray(byte.astype(np.uint8).reshape(k // 512, 16, n))


def unpack_fp4(words, scales):
    g, _, n = scales.shape
    words = np.ascontiguousarray(words).reshape(g, 128, n, 2)
    nib = np.empty((g, 128, n, 4), np.uint8)
    nib[..., 0::2] = words & 0xF
    nib[..., 1::2] = words >> 4
    vals = E2M1[nib] * np.repeat(np.exp2(scales.astype(np.float64) - 127.0), 8, axis=1)[..., None]
    return vals.transpose(0, 1, 3, 2).reshape(g * 512, n)


def planes(y):
    n, m = y.shape
    v = y.astype(np.float32).astype(ml_dtypes.bfloat16).astype(np.float64).reshape(n // 32, 32, m)
    top = np.abs(v).max(1)
    byte = np.clip(np.where(top > 0, np.frexp(top)[1] - 1 + 127 - 7, 1), 1, 254)
    codes = (v * np.exp2(127.0 - byte)[:, None, :]).reshape(n, m).astype(np.float32).astype(ml_dtypes.float8_e4m3fn).view(np.uint8)
    words = codes.reshape(n // 512, 128, 4, m).transpose(0, 1, 3, 2)
    return np.ascontiguousarray(words), np.ascontiguousarray(byte.astype(np.uint8).reshape(n // 512, 16, m))


K, T, S, N, H, G, U = 512, 1024, 512, 512, 512, 2048, 1024


def setup_inputs():
    n = np.random.standard_normal
    s = mx_kscale(K)[:, None]
    u = mx_kscale(S)
    packed_xT = pack_weight(n((K, T)) * s)
    packed_w1 = pack_fp4(n((K, H)) / np.sqrt(K) / s)
    packed_dT = pack_weight(n((K, G)) / s)
    packed_w2 = pack_fp4(n((H, N)) / np.sqrt(H) / u[:, None])
    return {
        "x_words": packed_xT[0],
        "x_scales": packed_xT[1],
        "w1_words": packed_w1[0],
        "w1_scales": packed_w1[1],
        "gs": (np.random.uniform(0.5, 1.5, (K, 1)) * s).astype(np.float32),
        "d_words": packed_dT[0],
        "d_scales": packed_dT[1],
        "mem": n((H, U)).astype(np.float32),
        "res": (1.5 * n((N, U))).astype(np.float32),
        "gn": (np.random.uniform(0.5, 1.5, (H, 1)) * u[:, None]).astype(np.float32),
        "w2_words": packed_w2[0],
        "w2_scales": packed_w2[1],
        "offs": striped(np.random.permutation(T)[:S]),
        "n1": striped8(np.stack([np.random.permutation(S) for _ in range(8)])),
        "n2": striped8(np.stack([np.random.permutation(S) for _ in range(8)])),
        "n3": striped8(np.stack([np.random.permutation(S) for _ in range(8)])),
        "kidx": striped8(np.random.randint(0, G, (8, H))),
        "n4": striped8(np.stack([np.random.permutation(U)[:S] for _ in range(8)])),
    }


def reference(x_words, x_scales, w1_words, w1_scales, gs, d_words, d_scales, mem, res, gn, w2_words, w2_scales, offs, n1, n2, n3, kidx, n4):
    d_kidx = unpack_weight(d_words, d_scales)[np.arange(K)[:, None], runs(kidx, K)]
    xq = unpack_weight(x_words, x_scales)[:, unstriped(offs)]
    y = unpack_fp4(w1_words, w1_scales).T @ xq
    z = f64(gs) * (np.maximum(y, y[np.arange(H)[:, None], runs(n1, H)]) - (np.maximum(y[np.arange(H)[:, None], runs(n2, H)], y[np.arange(H)[:, None], runs(n3, H)])))
    s = 0.0625 * ((d_kidx.T @ mxq(z, 0, "e4m3")))
    nw = np.maximum(s, 0.5 * (f64(mem)[np.arange(H)[:, None], runs(n4, H)]))
    pg = f64(mem).copy()
    pg[np.arange(H)[:, None], runs(n4, H)] = nw
    z2 = f64(gn) * pg
    out_0 = f64(res) + (unpack_fp4(w2_words, w2_scales).T @ mxq(z2, 0, "e4m3"))
    return (out_0,) + planes(out_0)

@@ -1,0 +1,255 @@
+from contextlib import ExitStack
+
+import concourse.mybir as mybir
+
+K, T, S, N, H, G, U = 512, 1024, 512, 512, 512, 2048, 1024
+FLOPS = 2 * K * H * S + 2 * K * H * S + 2 * H * N * U
+
+F32 = mybir.dt.float32
+BF16 = mybir.dt.bfloat16
+I32 = mybir.dt.int32
+U32 = mybir.dt.uint32
+U16 = mybir.dt.uint16
+U8 = mybir.dt.uint8
+FP8X4 = mybir.dt.float8_e4m3fn_x4
+FP4X4 = mybir.dt.float4_e2m1fn_x4
+ALU = mybir.AluOpType
+COPY = mybir.ActivationFunctionType.Copy
+
+P = 128
+PACK = 4
+QUADRANT = 32
+CHUNK = 256
+
+
+def tile_picked_pqkmixpagex_none_po_kernel(
+    tc, x_words, x_scales, w1_words, w1_scales, gs, d_words, d_scales, mem, res, gn,
+    w2_words, w2_scales, offs, n1, n2, n3, kidx, n4, out_0, out_1, out_2,
+):
+    nc = tc.nc
+    with ExitStack() as ctx:
+        keep = ctx.enter_context(tc.tile_pool(name="keep", bufs=1))
+        psum = ctx.enter_context(tc.psum_pool(name="psum", bufs=1))
+
+        def load_list(src, name):
+            tile = keep.tile([P, S // 16], U16, name=name)
+            nc.sync.dma_start(tile[:], src)
+            return tile
+
+        def load_words(src, width, name):
+            tile = keep.tile([P, width], U32, name=name, align_bytes=64)
+            nc.sync.dma_start(tile[:].bitcast(I32), src[0].rearrange("p n t -> p (n t)").bitcast(I32))
+            return tile
+
+        def load_fp4(src, name):
+            tile = keep.tile([P, 2 * H], U8, name=name, align_bytes=64)
+            nc.sync.dma_start(tile[:].bitcast(I32), src[0].bitcast(I32))
+            return tile
+
+        def load_scale_rows(src, width, name):
+            tile = keep.tile([P, width], U8, name=name, align_bytes=64)
+            rows = src[0].bitcast(I32)
+            for q in range(P // QUADRANT):
+                nc.sync.dma_start(
+                    tile[QUADRANT * q : QUADRANT * (q + 1), :].bitcast(I32),
+                    rows[4 * q : 4 * q + 4, :].unsqueeze(0).broadcast_to([8, 4, width // 4]),
+                )
+            return tile
+
+        def load_column(src, name):
+            tile = keep.tile([P, PACK], F32, name=name)
+            nc.sync.dma_start(tile[:], src.rearrange("(p t) o -> p (t o)", t=PACK))
+            return tile
+
+        def deal(dst, src, unit):
+            nc.vector.tensor_copy(
+                dst.rearrange("p (t m b) -> p t m b", t=PACK, b=unit),
+                src.rearrange("p (m t b) -> p t m b", t=PACK, b=unit),
+            )
+
+        offs_sb = load_list(offs, "offs_sb")
+        xw = load_words(x_words, T, "xw")
+        xs = load_scale_rows(x_scales, T, "xs")
+        w1w = load_fp4(w1_words, "w1w")
+        kidx_sb = load_list(kidx, "kidx_sb")
+        w1s = load_scale_rows(w1_scales, H, "w1s")
+        ds = keep.tile([P, G], U8, name="ds", align_bytes=64)
+        nc.sync.dma_start(
+            ds[:].bitcast(I32), d_scales[0].bitcast(I32).unsqueeze(1).broadcast_to([16, 8, G // 4])
+        )
+        dw = load_words(d_words, G, "dw")
+        n1_sb = load_list(n1, "n1_sb")
+        n2_sb = load_list(n2, "n2_sb")
+        n3_sb = load_list(n3, "n3_sb")
+        gs_sb = load_column(gs, "gs_sb")
+        page = []
+        for t in range(PACK):
+            tile = keep.tile([P, U], F32, name=f"page{t}")
+            nc.sync.dma_start(tile[:], mem.rearrange("(p t) w -> p t w", t=PACK)[:, t, :])
+            page.append(tile)
+        n4_sb = load_list(n4, "n4_sb")
+        gn_sb = load_column(gn, "gn_sb")
+        w2w = load_fp4(w2_words, "w2w")
+        w2s = load_scale_rows(w2_scales, N, "w2s")
+        res_sb = keep.tile([P, PACK, U], F32, name="res_sb")
+        nc.sync.dma_start(res_sb[:], res.rearrange("(p t) w -> p t w", t=PACK))
+
+        zero = keep.tile([P, 1], F32, name="zero")
+        nc.vector.memset(zero[:], 0.0)
+        ywin = []
+        for t in range(PACK):
+            tile = keep.tile([P, 2 * S], F32, name=f"ywin{t}")
+            nc.scalar.activation(tile[:, S:], zero[:].to_broadcast([P, S]), COPY)
+            ywin.append(tile)
+
+        w1w_d = keep.tile([P, 2 * H], U8, name="w1w_d", align_bytes=64)
+        deal(w1w_d[:], w1w[:], 2)
+        xq_s = keep.tile([P, S], U8, name="xq_s", align_bytes=64)
+        nc.vector.tensor_copy(xq_s[:], xs[:].indirect(offs_sb[:]))
+        xq_w = keep.tile([P, S], U32, name="xq_w", align_bytes=64)
+        nc.vector.tensor_copy(xq_w[:], xw[:].indirect(offs_sb[:]))
+        w1s_d = keep.tile([P, H], U8, name="w1s_d", align_bytes=64)
+        deal(w1s_d[:], w1s[:], 1)
+        for t in range(PACK):
+            bank = psum.tile([P, S], F32, name=f"y_bank{t}", tag=f"bank{t}")
+            nc.tensor.matmul_mx(
+                out=bank[:],
+                lhsT=w1w_d[:, 2 * P * t : 2 * P * (t + 1)].bitcast(FP4X4),
+                lhsT_scale=w1s_d[:, P * t : P * (t + 1)],
+                rhs=xq_w[:].bitcast(FP8X4),
+                rhs_scale=xq_s[:],
+                start=True,
+                stop=True,
+            )
+            nc.scalar.activation(ywin[t][:, :S], bank[:], COPY)
+
+        dq_s = keep.tile([P, H], U8, name="dq_s", align_bytes=64)
+        nc.vector.tensor_copy(dq_s[:], ds[:].indirect(kidx_sb[:]))
+        dq_w = keep.tile([P, H], U32, name="dq_w", align_bytes=64)
+        nc.vector.tensor_copy(dq_w[:], dw[:].indirect(kidx_sb[:]))
+        dq_s_d = keep.tile([P, H], U8, name="dq_s_d", align_bytes=64)
+        deal(dq_s_d[:], dq_s[:], 1)
+        dq_w_d = keep.tile([P, H], U32, name="dq_w_d", align_bytes=64)
+        deal(dq_w_d[:].bitcast(I32), dq_w[:].bitcast(I32), 1)
+        key_s = keep.tile([P, H], U8, name="key_s", align_bytes=64)
+        nc.gpsimd.memset(key_s[:], 0)
+        for r in range(4):
+            nc.sync.dma_start(
+                key_s[r:P:QUADRANT, :].bitcast(I32), dq_s_d[8 * r : P : QUADRANT, :].bitcast(I32)
+            )
+
+        z_bf = keep.tile([P, S, PACK], BF16, name="z_bf", tag="z_bf", align_bytes=64)
+
+        def fetch(t, lst, name):
+            tile = keep.tile([P, S], F32, name=f"{name}{t}", tag=f"{name}{t}")
+            nc.vector.tensor_copy(tile[:], ywin[t][:].indirect(lst[:]))
+            return tile
+
+        for t in range(PACK):
+            g1 = fetch(t, n1_sb, "ga")
+            g2 = fetch(t, n2_sb, "gb")
+            m1 = keep.tile([P, S], F32, name=f"ma{t}", tag=f"ma{t}")
+            nc.vector.tensor_tensor(m1[:], g1[:], ywin[t][:, :S], ALU.max)
+            g3 = fetch(t, n3_sb, "gc")
+            m2 = keep.tile([P, S], F32, name=f"mb{t}", tag=f"mb{t}")
+            nc.vector.tensor_tensor(m2[:], g2[:], g3[:], ALU.max)
+            diff = keep.tile([P, S], F32, name=f"diff{t}", tag=f"diff{t}")
+            nc.vector.tensor_tensor(diff[:], m1[:], m2[:], ALU.subtract)
+            nc.scalar.activation(z_bf[:, :, t], diff[:], COPY, scale=gs_sb[:, t : t + 1])
+
+        half_old = []
+        for t, tag in enumerate(("ga3", "gb3", "gc3", "ma3")):
+            tile = keep.tile([P, S], F32, name=f"half_old{t}", tag=tag)
+            nc.vector.tensor_scalar(tile[:], page[t][:].indirect(n4_sb[:]), 0.5, 0.0, ALU.mult, ALU.add)
+            half_old.append(tile)
+
+        z_w = keep.tile([P, S], U32, name="z_w", align_bytes=64)
+        z_s = keep.tile([P, S], U8, name="z_s", align_bytes=64)
+        nc.vector.quantize_mx(
+            out=z_w[:].bitcast(FP8X4), scales=z_s[:], in_=z_bf[:].rearrange("p c t -> p (c t)")
+        )
+
+        w2w_d = keep.tile([P, 2 * N], U8, name="w2w_d", tag="z_bf", align_bytes=64)
+        deal(w2w_d[:], w2w[:], 2)
+        w2s_d = keep.tile([P, N], U8, name="w2s_d", align_bytes=64)
+        deal(w2s_d[:], w2s[:], 1)
+
+        z2_bf = [
+            keep.tile([P, CHUNK, PACK], BF16, name=f"z2_bf{c}", align_bytes=64) for c in range(U // CHUNK)
+        ]
+        for t in range(PACK):
+            bank = psum.tile([P, S], F32, name=f"s_bank{t}", tag=f"bank{PACK + t}")
+            nc.tensor.matmul_mx(
+                out=bank[:],
+                lhsT=dq_w_d[:, P * t : P * (t + 1)].bitcast(FP8X4),
+                lhsT_scale=key_s[:, P * t : P * (t + 1)],
+                rhs=z_w[:].bitcast(FP8X4),
+                rhs_scale=z_s[:],
+                start=True,
+                stop=True,
+            )
+            new = keep.tile([P, S], F32, name=f"new{t}")
+            nc.vector.scalar_tensor_tensor(new[:], bank[:], 0.0625, half_old[t][:], ALU.mult, ALU.max)
+            nc.vector.tensor_copy(page[t][:].indirect(n4_sb[:]), new[:])
+            for c in range(U // CHUNK):
+                nc.scalar.activation(
+                    z2_bf[c][:, :, t], page[t][:, CHUNK * c : CHUNK * (c + 1)], COPY, scale=gn_sb[:, t : t + 1]
+                )
+
+        out_rows = out_0.rearrange("(p t) w -> p t w", t=PACK)
+        out_words = out_1[0].rearrange("p n t -> p (n t)").bitcast(I32)
+        o_s = keep.tile([P, U], U8, name="o_s", align_bytes=64)
+        chunks = range(U // CHUNK)
+        z2_w, z2_s, y_out, o_bf = {}, {}, {}, {}
+
+        def quantise_page(c):
+            z2_w[c] = keep.tile([P, CHUNK], U32, name=f"z2_w{c}", align_bytes=64)
+            z2_s[c] = keep.tile([P, CHUNK], U8, name=f"z2_s{c}", align_bytes=64)
+            nc.vector.quantize_mx(
+                out=z2_w[c][:].bitcast(FP8X4), scales=z2_s[c][:], in_=z2_bf[c][:].rearrange("p c t -> p (c t)")
+            )
+
+        def product(c):
+            cols = slice(CHUNK * c, CHUNK * (c + 1))
+            y_out[c] = keep.tile([P, PACK, CHUNK], F32, name=f"y_out{c}")
+            for pair in range(PACK // 2):
+                bank = psum.tile([P, 2, CHUNK], F32, name=f"o_bank{c}_{pair}", tag=f"bank{2 * c + pair}")
+                for e in range(2):
+                    t = 2 * pair + e
+                    nc.tensor.matmul_mx(
+                        out=bank[:, e, :],
+                        lhsT=w2w_d[:, 2 * P * t : 2 * P * (t + 1)].bitcast(FP4X4),
+                        lhsT_scale=w2s_d[:, P * t : P * (t + 1)],
+                        rhs=z2_w[c][:].bitcast(FP8X4),
+                        rhs_scale=z2_s[c][:],
+                        start=True,
+                        stop=True,
+                    )
+                rows = slice(2 * pair, 2 * pair + 2)
+                nc.vector.tensor_tensor(y_out[c][:, rows, :], bank[:], res_sb[:, rows, cols], ALU.add)
+            nc.sync.dma_start(out_rows[:, :, cols], y_out[c][:])
+            o_bf[c] = keep.tile([P, CHUNK, PACK], BF16, name=f"o_bf{c}", align_bytes=64)
+            nc.scalar.activation(o_bf[c][:], y_out[c][:].rearrange("p t c -> p c t"), COPY)
+
+        def quantise_out(c):
+            cols = slice(CHUNK * c, CHUNK * (c + 1))
+            o_w = keep.tile([P, CHUNK], U32, name=f"o_w{c}", align_bytes=64)
+            nc.vector.quantize_mx(
+                out=o_w[:].bitcast(FP8X4), scales=o_s[:, cols], in_=o_bf[c][:].rearrange("p c t -> p (c t)")
+            )
+            nc.sync.dma_start(out_words[:, cols], o_w[:].bitcast(I32))
+
+        quantise_page(0)
+        for c in chunks:
+            if c + 1 in chunks:
+                quantise_page(c + 1)
+            product(c)
+            if c - 2 in chunks:
+                quantise_out(c - 2)
+        quantise_out(2)
+        quantise_out(3)
+        out_scales = out_2[0].bitcast(I32)
+        for q in range(P // QUADRANT):
+            nc.scalar.dma_start(
+                out_scales[4 * q : 4 * q + 4, :], o_s[QUADRANT * q : QUADRANT * q + 4, :].bitcast(I32)
+            )

@@ -19,7 +19,9 @@ COPY = mybir.ActivationFunctionType.Copy
 P = 128
 PACK = 4
 QUADRANT = 32
-CHUNK = 256
+BANK = 512
+WIDTHS = (128, 128, 256, 256, 256)
+STARTS = tuple(sum(WIDTHS[:c]) for c in range(len(WIDTHS)))
 
 
 def tile_picked_pqkmixpagex_none_po_kernel(
@@ -67,10 +69,10 @@ def tile_picked_pqkmixpagex_none_po_kernel(
                 src.rearrange("p (m t b) -> p t m b", t=PACK, b=unit),
             )
 
-        offs_sb = load_list(offs, "offs_sb")
-        xw = load_words(x_words, T, "xw")
-        xs = load_scale_rows(x_scales, T, "xs")
         w1w = load_fp4(w1_words, "w1w")
+        offs_sb = load_list(offs, "offs_sb")
+        xs = load_scale_rows(x_scales, T, "xs")
+        xw = load_words(x_words, T, "xw")
         kidx_sb = load_list(kidx, "kidx_sb")
         w1s = load_scale_rows(w1_scales, H, "w1s")
         ds = keep.tile([P, G], U8, name="ds", align_bytes=64)
@@ -140,25 +142,38 @@ def tile_picked_pqkmixpagex_none_po_kernel(
 
         z_bf = keep.tile([P, S, PACK], BF16, name="z_bf", tag="z_bf", align_bytes=64)
 
-        def fetch(t, lst, name):
+        neg_gs = keep.tile([P, PACK], F32, name="neg_gs")
+        nc.scalar.activation(neg_gs[:], gs_sb[:], COPY, scale=-1.0)
+        own, top = {}, {}
+
+        def fetch_own(t):
+            own[t] = keep.tile([P, S], F32, name=f"ga{t}", tag=f"ga{t}")
+            nc.vector.tensor_copy(own[t][:], ywin[t][:].indirect(n1_sb[:]))
+
+        def top_of(t):
+            top[t] = keep.tile([P, S], F32, name=f"ma{t}", tag=f"ma{t}")
+            nc.vector.tensor_tensor(top[t][:], own[t][:], ywin[t][:, :S], ALU.max)
+
+        def fetch_less(t, lst, name):
             tile = keep.tile([P, S], F32, name=f"{name}{t}", tag=f"{name}{t}")
-            nc.vector.tensor_copy(tile[:], ywin[t][:].indirect(lst[:]))
+            nc.vector.tensor_tensor(tile[:], ywin[t][:].indirect(lst[:]), top[t][:], ALU.subtract)
             return tile
 
+        fetch_own(0)
+        top_of(0)
         for t in range(PACK):
-            g1 = fetch(t, n1_sb, "ga")
-            g2 = fetch(t, n2_sb, "gb")
-            m1 = keep.tile([P, S], F32, name=f"ma{t}", tag=f"ma{t}")
-            nc.vector.tensor_tensor(m1[:], g1[:], ywin[t][:, :S], ALU.max)
-            g3 = fetch(t, n3_sb, "gc")
-            m2 = keep.tile([P, S], F32, name=f"mb{t}", tag=f"mb{t}")
-            nc.vector.tensor_tensor(m2[:], g2[:], g3[:], ALU.max)
+            if t + 1 < PACK:
+                fetch_own(t + 1)
+            e = fetch_less(t, n2_sb, "gb")
+            f = fetch_less(t, n3_sb, "gc")
+            if t + 1 < PACK:
+                top_of(t + 1)
             diff = keep.tile([P, S], F32, name=f"diff{t}", tag=f"diff{t}")
-            nc.vector.tensor_tensor(diff[:], m1[:], m2[:], ALU.subtract)
-            nc.scalar.activation(z_bf[:, :, t], diff[:], COPY, scale=gs_sb[:, t : t + 1])
+            nc.vector.tensor_tensor(diff[:], e[:], f[:], ALU.max)
+            nc.scalar.activation(z_bf[:, :, t], diff[:], COPY, scale=neg_gs[:, t : t + 1])
 
         half_old = []
-        for t, tag in enumerate(("ga3", "gb3", "gc3", "ma3")):
+        for t, tag in enumerate(("ma3", "gb3", "gc3", "diff3")):
             tile = keep.tile([P, S], F32, name=f"half_old{t}", tag=tag)
             nc.vector.tensor_scalar(tile[:], page[t][:].indirect(n4_sb[:]), 0.5, 0.0, ALU.mult, ALU.add)
             half_old.append(tile)
@@ -174,9 +189,9 @@ def tile_picked_pqkmixpagex_none_po_kernel(
         w2s_d = keep.tile([P, N], U8, name="w2s_d", align_bytes=64)
         deal(w2s_d[:], w2s[:], 1)
 
-        z2_bf = [
-            keep.tile([P, CHUNK, PACK], BF16, name=f"z2_bf{c}", align_bytes=64) for c in range(U // CHUNK)
-        ]
+        chunks = range(len(WIDTHS))
+        cols = [slice(STARTS[c], STARTS[c] + WIDTHS[c]) for c in chunks]
+        z2_bf = [keep.tile([P, WIDTHS[c], PACK], BF16, name=f"z2_bf{c}", align_bytes=64) for c in chunks]
         for t in range(PACK):
             bank = psum.tile([P, S], F32, name=f"s_bank{t}", tag=f"bank{PACK + t}")
             nc.tensor.matmul_mx(
@@ -191,31 +206,31 @@ def tile_picked_pqkmixpagex_none_po_kernel(
             new = keep.tile([P, S], F32, name=f"new{t}")
             nc.vector.scalar_tensor_tensor(new[:], bank[:], 0.0625, half_old[t][:], ALU.mult, ALU.max)
             nc.vector.tensor_copy(page[t][:].indirect(n4_sb[:]), new[:])
-            for c in range(U // CHUNK):
-                nc.scalar.activation(
-                    z2_bf[c][:, :, t], page[t][:, CHUNK * c : CHUNK * (c + 1)], COPY, scale=gn_sb[:, t : t + 1]
-                )
+            for c in chunks:
+                nc.scalar.activation(z2_bf[c][:, :, t], page[t][:, cols[c]], COPY, scale=gn_sb[:, t : t + 1])
 
         out_rows = out_0.rearrange("(p t) w -> p t w", t=PACK)
         out_words = out_1[0].rearrange("p n t -> p (n t)").bitcast(I32)
         o_s = keep.tile([P, U], U8, name="o_s", align_bytes=64)
-        chunks = range(U // CHUNK)
         z2_w, z2_s, y_out, o_bf = {}, {}, {}, {}
+        last = len(WIDTHS) - 1
 
         def quantise_page(c):
-            z2_w[c] = keep.tile([P, CHUNK], U32, name=f"z2_w{c}", align_bytes=64)
-            z2_s[c] = keep.tile([P, CHUNK], U8, name=f"z2_s{c}", align_bytes=64)
+            z2_w[c] = keep.tile([P, WIDTHS[c]], U32, name=f"z2_w{c}", align_bytes=64)
+            z2_s[c] = keep.tile([P, WIDTHS[c]], U8, name=f"z2_s{c}", align_bytes=64)
             nc.vector.quantize_mx(
                 out=z2_w[c][:].bitcast(FP8X4), scales=z2_s[c][:], in_=z2_bf[c][:].rearrange("p c t -> p (c t)")
             )
 
         def product(c):
-            cols = slice(CHUNK * c, CHUNK * (c + 1))
-            y_out[c] = keep.tile([P, PACK, CHUNK], F32, name=f"y_out{c}")
-            for pair in range(PACK // 2):
-                bank = psum.tile([P, 2, CHUNK], F32, name=f"o_bank{c}_{pair}", tag=f"bank{2 * c + pair}")
-                for e in range(2):
-                    t = 2 * pair + e
+            width = WIDTHS[c]
+            per_bank = BANK // width
+            y_out[c] = keep.tile([P, PACK, width], F32, name=f"y_out{c}")
+            for b in range(PACK // per_bank):
+                number = PACK * STARTS[c] // BANK + b
+                bank = psum.tile([P, per_bank, width], F32, name=f"o_bank{number}", tag=f"bank{number}")
+                for e in range(per_bank):
+                    t = per_bank * b + e
                     nc.tensor.matmul_mx(
                         out=bank[:, e, :],
                         lhsT=w2w_d[:, 2 * P * t : 2 * P * (t + 1)].bitcast(FP4X4),
@@ -225,31 +240,35 @@ def tile_picked_pqkmixpagex_none_po_kernel(
                         start=True,
                         stop=True,
                     )
-                rows = slice(2 * pair, 2 * pair + 2)
-                nc.vector.tensor_tensor(y_out[c][:, rows, :], bank[:], res_sb[:, rows, cols], ALU.add)
-            nc.sync.dma_start(out_rows[:, :, cols], y_out[c][:])
-            o_bf[c] = keep.tile([P, CHUNK, PACK], BF16, name=f"o_bf{c}", align_bytes=64)
-            nc.scalar.activation(o_bf[c][:], y_out[c][:].rearrange("p t c -> p c t"), COPY)
+                rows = slice(per_bank * b, per_bank * (b + 1))
+                nc.vector.tensor_tensor(y_out[c][:, rows, :], bank[:], res_sb[:, rows, cols[c]], ALU.add)
+            nc.sync.dma_start(out_rows[:, :, cols[c]], y_out[c][:])
+            o_bf[c] = keep.tile([P, width, PACK], BF16, name=f"o_bf{c}", align_bytes=64)
+            grouped = y_out[c][:].rearrange("p t c -> p c t")
+            split = width // 2 if c == last else width
+            nc.scalar.activation(o_bf[c][:, :split, :], grouped[:, :split, :], COPY)
+            return grouped, split
 
         def quantise_out(c):
-            cols = slice(CHUNK * c, CHUNK * (c + 1))
-            o_w = keep.tile([P, CHUNK], U32, name=f"o_w{c}", align_bytes=64)
+            o_w = keep.tile([P, WIDTHS[c]], U32, name=f"o_w{c}", align_bytes=64)
             nc.vector.quantize_mx(
-                out=o_w[:].bitcast(FP8X4), scales=o_s[:, cols], in_=o_bf[c][:].rearrange("p c t -> p (c t)")
+                out=o_w[:].bitcast(FP8X4), scales=o_s[:, cols[c]], in_=o_bf[c][:].rearrange("p c t -> p (c t)")
             )
-            nc.sync.dma_start(out_words[:, cols], o_w[:].bitcast(I32))
+            nc.sync.dma_start(out_words[:, cols[c]], o_w[:].bitcast(I32))
 
         quantise_page(0)
         for c in chunks:
             if c + 1 in chunks:
                 quantise_page(c + 1)
-            product(c)
+            grouped, split = product(c)
             if c - 2 in chunks:
                 quantise_out(c - 2)
-        quantise_out(2)
-        quantise_out(3)
+        nc.vector.tensor_copy(o_bf[last][:, split:, :], grouped[:, split:, :])
+        quantise_out(last - 1)
+        quantise_out(last)
         out_scales = out_2[0].bitcast(I32)
         for q in range(P // QUADRANT):
-            nc.scalar.dma_start(
+            queue = nc.scalar if q % 2 == 0 else nc.sync
+            queue.dma_start(
                 out_scales[4 * q : 4 * q + 4, :], o_s[QUADRANT * q : QUADRANT * q + 4, :].bitcast(I32)
             )

@@ -20,7 +20,9 @@ P = 128
 PACK = 4
 QUADRANT = 32
 BANK = 512
-WIDTHS = (128, 128, 256, 256, 256)
+BLOCK = BANK // PACK
+STORE = 256
+WIDTHS = (128, 256, 256, 256, 128)
 STARTS = tuple(sum(WIDTHS[:c]) for c in range(len(WIDTHS)))
 
 
@@ -132,7 +134,10 @@ def tile_picked_pqkmixpagex_none_po_kernel(
         dq_s_d = keep.tile([P, H], U8, name="dq_s_d", align_bytes=64)
         deal(dq_s_d[:], dq_s[:], 1)
         dq_w_d = keep.tile([P, H], U32, name="dq_w_d", align_bytes=64)
-        deal(dq_w_d[:].bitcast(I32), dq_w[:].bitcast(I32), 1)
+        nc.vector.tensor_copy(
+            dq_w_d[:].bitcast(I32).rearrange("p (t m) -> p m t", t=PACK),
+            dq_w[:].bitcast(I32).rearrange("p (m t) -> p m t", t=PACK),
+        )
         key_s = keep.tile([P, H], U8, name="key_s", align_bytes=64)
         nc.gpsimd.memset(key_s[:], 0)
         for r in range(4):
@@ -191,8 +196,11 @@ def tile_picked_pqkmixpagex_none_po_kernel(
 
         chunks = range(len(WIDTHS))
         cols = [slice(STARTS[c], STARTS[c] + WIDTHS[c]) for c in chunks]
-        z2_bf = [keep.tile([P, WIDTHS[c], PACK], BF16, name=f"z2_bf{c}", align_bytes=64) for c in chunks]
-        for t in range(PACK):
+        z2_bf = keep.tile([P, U * PACK], BF16, name="z2_bf", align_bytes=64)
+        z2_planes = z2_bf[:].rearrange("p (c t) -> p c t", t=PACK)
+        new = []
+
+        def score(t):
             bank = psum.tile([P, S], F32, name=f"s_bank{t}", tag=f"bank{PACK + t}")
             nc.tensor.matmul_mx(
                 out=bank[:],
@@ -203,69 +211,88 @@ def tile_picked_pqkmixpagex_none_po_kernel(
                 start=True,
                 stop=True,
             )
-            new = keep.tile([P, S], F32, name=f"new{t}")
-            nc.vector.scalar_tensor_tensor(new[:], bank[:], 0.0625, half_old[t][:], ALU.mult, ALU.max)
-            nc.vector.tensor_copy(page[t][:].indirect(n4_sb[:]), new[:])
-            for c in chunks:
-                nc.scalar.activation(z2_bf[c][:, :, t], page[t][:, cols[c]], COPY, scale=gn_sb[:, t : t + 1])
+            tile = keep.tile([P, S], F32, name=f"new{t}")
+            nc.vector.scalar_tensor_tensor(tile[:], bank[:], 0.0625, half_old[t][:], ALU.mult, ALU.max)
+            new.append(tile)
+
+        def weigh_on_scalar(t, span):
+            nc.scalar.activation(z2_planes[:, span, t], page[t][:, span], COPY, scale=gn_sb[:, t : t + 1])
+
+        score(0)
+        for t in range(PACK):
+            if t + 1 < PACK:
+                score(t + 1)
+            nc.vector.tensor_copy(page[t][:].indirect(n4_sb[:]), new[t][:])
+            if t < 2:
+                weigh_on_scalar(t, slice(0, U))
+            elif t == 2:
+                weigh_on_scalar(t, slice(WIDTHS[0], U))
+        for t in (2, 3):
+            nc.vector.tensor_scalar(
+                z2_planes[:, cols[0], t], page[t][:, cols[0]], gn_sb[:, t : t + 1], None, ALU.mult
+            )
+        for c in chunks[1:]:
+            weigh_on_scalar(3, cols[c])
 
         out_rows = out_0.rearrange("(p t) w -> p t w", t=PACK)
         out_words = out_1[0].rearrange("p n t -> p (n t)").bitcast(I32)
+        o_w = keep.tile([P, U], U32, name="o_w", align_bytes=64)
         o_s = keep.tile([P, U], U8, name="o_s", align_bytes=64)
-        z2_w, z2_s, y_out, o_bf = {}, {}, {}, {}
-        last = len(WIDTHS) - 1
+        z2_w = keep.tile([P, U], U32, name="z2_w", align_bytes=64)
+        z2_s = keep.tile([P, U], U8, name="z2_s", align_bytes=64)
+        y_out = [keep.tile([P, PACK, STORE], F32, name=f"y_out{g}") for g in range(U // STORE)]
+        o_bf = [keep.tile([P, STORE, PACK], BF16, name=f"o_bf{g}", align_bytes=64) for g in range(U // STORE)]
 
         def quantise_page(c):
-            z2_w[c] = keep.tile([P, WIDTHS[c]], U32, name=f"z2_w{c}", align_bytes=64)
-            z2_s[c] = keep.tile([P, WIDTHS[c]], U8, name=f"z2_s{c}", align_bytes=64)
             nc.vector.quantize_mx(
-                out=z2_w[c][:].bitcast(FP8X4), scales=z2_s[c][:], in_=z2_bf[c][:].rearrange("p c t -> p (c t)")
+                out=z2_w[:, cols[c]].bitcast(FP8X4),
+                scales=z2_s[:, cols[c]],
+                in_=z2_bf[:, PACK * STARTS[c] : PACK * (STARTS[c] + WIDTHS[c])],
             )
 
-        def product(c):
-            width = WIDTHS[c]
-            per_bank = BANK // width
-            y_out[c] = keep.tile([P, PACK, width], F32, name=f"y_out{c}")
-            for b in range(PACK // per_bank):
-                number = PACK * STARTS[c] // BANK + b
-                bank = psum.tile([P, per_bank, width], F32, name=f"o_bank{number}", tag=f"bank{number}")
-                for e in range(per_bank):
-                    t = per_bank * b + e
-                    nc.tensor.matmul_mx(
-                        out=bank[:, e, :],
-                        lhsT=w2w_d[:, 2 * P * t : 2 * P * (t + 1)].bitcast(FP4X4),
-                        lhsT_scale=w2s_d[:, P * t : P * (t + 1)],
-                        rhs=z2_w[c][:].bitcast(FP8X4),
-                        rhs_scale=z2_s[c][:],
-                        start=True,
-                        stop=True,
-                    )
-                rows = slice(per_bank * b, per_bank * (b + 1))
-                nc.vector.tensor_tensor(y_out[c][:, rows, :], bank[:], res_sb[:, rows, cols[c]], ALU.add)
-            nc.sync.dma_start(out_rows[:, :, cols[c]], y_out[c][:])
-            o_bf[c] = keep.tile([P, width, PACK], BF16, name=f"o_bf{c}", align_bytes=64)
-            grouped = y_out[c][:].rearrange("p t c -> p c t")
-            split = width // 2 if c == last else width
-            nc.scalar.activation(o_bf[c][:, :split, :], grouped[:, :split, :], COPY)
-            return grouped, split
-
-        def quantise_out(c):
-            o_w = keep.tile([P, WIDTHS[c]], U32, name=f"o_w{c}", align_bytes=64)
-            nc.vector.quantize_mx(
-                out=o_w[:].bitcast(FP8X4), scales=o_s[:, cols[c]], in_=o_bf[c][:].rearrange("p c t -> p (c t)")
+        def product(b):
+            block = slice(BLOCK * b, BLOCK * (b + 1))
+            g, part = divmod(BLOCK * b, STORE)
+            inside = slice(part, part + BLOCK)
+            bank = psum.tile([P, PACK, BLOCK], F32, name=f"o_bank{b}", tag=f"bank{b}")
+            for t in range(PACK):
+                nc.tensor.matmul_mx(
+                    out=bank[:, t, :],
+                    lhsT=w2w_d[:, 2 * P * t : 2 * P * (t + 1)].bitcast(FP4X4),
+                    lhsT_scale=w2s_d[:, P * t : P * (t + 1)],
+                    rhs=z2_w[:, block].bitcast(FP8X4),
+                    rhs_scale=z2_s[:, block],
+                    start=True,
+                    stop=True,
+                )
+            nc.vector.tensor_tensor(y_out[g][:, :, inside], bank[:], res_sb[:, :, block], ALU.add)
+            nc.scalar.activation(
+                o_bf[g][:, inside, :].rearrange("p (c i) t -> p c t i", i=4),
+                y_out[g][:, :, inside].rearrange("p t (c i) -> p c t i", i=4),
+                COPY,
             )
-            nc.sync.dma_start(out_words[:, cols[c]], o_w[:].bitcast(I32))
+            if part + BLOCK == STORE:
+                nc.sync.dma_start(out_rows[:, :, STORE * g : STORE * (g + 1)], y_out[g][:])
+
+        def quantise_out(g):
+            span = slice(STORE * g, STORE * (g + 1))
+            nc.vector.quantize_mx(
+                out=o_w[:, span].bitcast(FP8X4), scales=o_s[:, span], in_=o_bf[g][:].rearrange("p c t -> p (c t)")
+            )
 
         quantise_page(0)
+        done = 0
         for c in chunks:
             if c + 1 in chunks:
                 quantise_page(c + 1)
-            grouped, split = product(c)
-            if c - 2 in chunks:
-                quantise_out(c - 2)
-        nc.vector.tensor_copy(o_bf[last][:, split:, :], grouped[:, split:, :])
-        quantise_out(last - 1)
-        quantise_out(last)
+            for b in range(done, done + WIDTHS[c] // BLOCK):
+                product(b)
+            done = done + WIDTHS[c] // BLOCK
+        for g in range(U // STORE - 1):
+            quantise_out(g)
+        nc.sync.dma_start(out_words[:, : U - STORE], o_w[:, : U - STORE].bitcast(I32))
+        quantise_out(U // STORE - 1)
+        nc.sync.dma_start(out_words[:, U - STORE :], o_w[:, U - STORE :].bitcast(I32))
         out_scales = out_2[0].bitcast(I32)
         for q in range(P // QUADRANT):
             queue = nc.scalar if q % 2 == 0 else nc.sync

@@ -65,15 +65,15 @@ def tile_picked_pqkmixpagex_none_po_kernel(
             nc.sync.dma_start(tile[:], src.rearrange("(p t) o -> p (t o)", t=PACK))
             return tile
 
-        def deal(dst, src, unit):
-            nc.vector.tensor_copy(
+        def deal(dst, src, unit, engine=nc.vector):
+            engine.tensor_copy(
                 dst.rearrange("p (t m b) -> p t m b", t=PACK, b=unit),
                 src.rearrange("p (m t b) -> p t m b", t=PACK, b=unit),
             )
 
-        w1w = load_fp4(w1_words, "w1w")
         offs_sb = load_list(offs, "offs_sb")
         xs = load_scale_rows(x_scales, T, "xs")
+        w1w = load_fp4(w1_words, "w1w")
         xw = load_words(x_words, T, "xw")
         kidx_sb = load_list(kidx, "kidx_sb")
         w1s = load_scale_rows(w1_scales, H, "w1s")
@@ -81,10 +81,10 @@ def tile_picked_pqkmixpagex_none_po_kernel(
         nc.sync.dma_start(
             ds[:].bitcast(I32), d_scales[0].bitcast(I32).unsqueeze(1).broadcast_to([16, 8, G // 4])
         )
-        dw = load_words(d_words, G, "dw")
         n1_sb = load_list(n1, "n1_sb")
         n2_sb = load_list(n2, "n2_sb")
         n3_sb = load_list(n3, "n3_sb")
+        dw = load_words(d_words, G, "dw")
         gs_sb = load_column(gs, "gs_sb")
         page = []
         for t in range(PACK):
@@ -107,13 +107,13 @@ def tile_picked_pqkmixpagex_none_po_kernel(
             ywin.append(tile)
 
         w1w_d = keep.tile([P, 2 * H], U8, name="w1w_d", align_bytes=64)
-        deal(w1w_d[:], w1w[:], 2)
+        deal(w1w_d[:], w1w[:], 2, nc.gpsimd)
         xq_s = keep.tile([P, S], U8, name="xq_s", align_bytes=64)
         nc.vector.tensor_copy(xq_s[:], xs[:].indirect(offs_sb[:]))
         xq_w = keep.tile([P, S], U32, name="xq_w", align_bytes=64)
         nc.vector.tensor_copy(xq_w[:], xw[:].indirect(offs_sb[:]))
         w1s_d = keep.tile([P, H], U8, name="w1s_d", align_bytes=64)
-        deal(w1s_d[:], w1s[:], 1)
+        deal(w1s_d[:], w1s[:], 1, nc.gpsimd)
         for t in range(PACK):
             bank = psum.tile([P, S], F32, name=f"y_bank{t}", tag=f"bank{t}")
             nc.tensor.matmul_mx(
@@ -130,25 +130,29 @@ def tile_picked_pqkmixpagex_none_po_kernel(
         dq_s = keep.tile([P, H], U8, name="dq_s", align_bytes=64)
         nc.vector.tensor_copy(dq_s[:], ds[:].indirect(kidx_sb[:]))
         dq_w = keep.tile([P, H], U32, name="dq_w", align_bytes=64)
-        nc.vector.tensor_copy(dq_w[:], dw[:].indirect(kidx_sb[:]))
         dq_s_d = keep.tile([P, H], U8, name="dq_s_d", align_bytes=64)
-        deal(dq_s_d[:], dq_s[:], 1)
         dq_w_d = keep.tile([P, H], U32, name="dq_w_d", align_bytes=64)
-        nc.vector.tensor_copy(
-            dq_w_d[:].bitcast(I32).rearrange("p (t m) -> p m t", t=PACK),
-            dq_w[:].bitcast(I32).rearrange("p (m t) -> p m t", t=PACK),
-        )
         key_s = keep.tile([P, H], U8, name="key_s", align_bytes=64)
         nc.gpsimd.memset(key_s[:], 0)
-        for r in range(4):
-            nc.sync.dma_start(
-                key_s[r:P:QUADRANT, :].bitcast(I32), dq_s_d[8 * r : P : QUADRANT, :].bitcast(I32)
+
+        def place_key_scales():
+            deal(dq_s_d[:], dq_s[:], 1)
+            for r in range(4):
+                nc.sync.dma_start(
+                    key_s[r:P:QUADRANT, :].bitcast(I32), dq_s_d[8 * r : P : QUADRANT, :].bitcast(I32)
+                )
+
+        def fetch_key_words():
+            nc.vector.tensor_copy(dq_w[:], dw[:].indirect(kidx_sb[:]))
+
+        def deal_key_words():
+            nc.vector.tensor_copy(
+                dq_w_d[:].bitcast(I32).rearrange("p (t m) -> p m t", t=PACK),
+                dq_w[:].bitcast(I32).rearrange("p (m t) -> p m t", t=PACK),
             )
 
         z_bf = keep.tile([P, S, PACK], BF16, name="z_bf", tag="z_bf", align_bytes=64)
 
-        neg_gs = keep.tile([P, PACK], F32, name="neg_gs")
-        nc.scalar.activation(neg_gs[:], gs_sb[:], COPY, scale=-1.0)
         own, top = {}, {}
 
         def fetch_own(t):
@@ -156,15 +160,23 @@ def tile_picked_pqkmixpagex_none_po_kernel(
             nc.vector.tensor_copy(own[t][:], ywin[t][:].indirect(n1_sb[:]))
 
         def top_of(t):
-            top[t] = keep.tile([P, S], F32, name=f"ma{t}", tag=f"ma{t}")
+            top[t] = keep.tile([P, S], F32, name=f"ma{t}", tag=f"ma{t}", align_bytes=64)
             nc.vector.tensor_tensor(top[t][:], own[t][:], ywin[t][:, :S], ALU.max)
 
         def fetch_less(t, lst, name):
-            tile = keep.tile([P, S], F32, name=f"{name}{t}", tag=f"{name}{t}")
+            tile = keep.tile([P, S], F32, name=f"{name}{t}", tag=f"{name}{t}", align_bytes=64)
             nc.vector.tensor_tensor(tile[:], ywin[t][:].indirect(lst[:]), top[t][:], ALU.subtract)
             return tile
 
+        half_old = []
+
+        def fetch_old(t, tag):
+            tile = keep.tile([P, S], F32, name=f"half_old{t}", tag=tag, align_bytes=64)
+            nc.vector.tensor_scalar(tile[:], page[t][:].indirect(n4_sb[:]), 0.5, 0.0, ALU.mult, ALU.add)
+            half_old.append(tile)
+
         fetch_own(0)
+        place_key_scales()
         top_of(0)
         for t in range(PACK):
             if t + 1 < PACK:
@@ -173,15 +185,17 @@ def tile_picked_pqkmixpagex_none_po_kernel(
             f = fetch_less(t, n3_sb, "gc")
             if t + 1 < PACK:
                 top_of(t + 1)
-            diff = keep.tile([P, S], F32, name=f"diff{t}", tag=f"diff{t}")
+            else:
+                fetch_old(0, "ma2")
+            diff = keep.tile([P, S], F32, name=f"diff{t}")
             nc.vector.tensor_tensor(diff[:], e[:], f[:], ALU.max)
-            nc.scalar.activation(z_bf[:, :, t], diff[:], COPY, scale=neg_gs[:, t : t + 1])
-
-        half_old = []
-        for t, tag in enumerate(("ma3", "gb3", "gc3", "diff3")):
-            tile = keep.tile([P, S], F32, name=f"half_old{t}", tag=tag)
-            nc.vector.tensor_scalar(tile[:], page[t][:].indirect(n4_sb[:]), 0.5, 0.0, ALU.mult, ALU.add)
-            half_old.append(tile)
+            nc.scalar.activation(z_bf[:, :, t], diff[:], COPY, scale=gs_sb[:, t : t + 1])
+            if t == 0:
+                fetch_key_words()
+            elif t == 1:
+                deal_key_words()
+        fetch_old(1, "ma3")
+        fetch_old(2, "gb3")
 
         z_w = keep.tile([P, S], U32, name="z_w", align_bytes=64)
         z_s = keep.tile([P, S], U8, name="z_s", align_bytes=64)
@@ -189,10 +203,8 @@ def tile_picked_pqkmixpagex_none_po_kernel(
             out=z_w[:].bitcast(FP8X4), scales=z_s[:], in_=z_bf[:].rearrange("p c t -> p (c t)")
         )
 
-        w2w_d = keep.tile([P, 2 * N], U8, name="w2w_d", tag="z_bf", align_bytes=64)
-        deal(w2w_d[:], w2w[:], 2)
-        w2s_d = keep.tile([P, N], U8, name="w2s_d", align_bytes=64)
-        deal(w2s_d[:], w2s[:], 1)
+
+        fetch_old(3, "z_bf")
 
         chunks = range(len(WIDTHS))
         cols = [slice(STARTS[c], STARTS[c] + WIDTHS[c]) for c in chunks]
@@ -212,7 +224,7 @@ def tile_picked_pqkmixpagex_none_po_kernel(
                 stop=True,
             )
             tile = keep.tile([P, S], F32, name=f"new{t}")
-            nc.vector.scalar_tensor_tensor(tile[:], bank[:], 0.0625, half_old[t][:], ALU.mult, ALU.max)
+            nc.vector.scalar_tensor_tensor(tile[:], bank[:], -0.0625, half_old[t][:], ALU.mult, ALU.max)
             new.append(tile)
 
         def weigh_on_scalar(t, span):
@@ -233,6 +245,11 @@ def tile_picked_pqkmixpagex_none_po_kernel(
             )
         for c in chunks[1:]:
             weigh_on_scalar(3, cols[c])
+
+        w2w_d = keep.tile([P, 2 * N], U8, name="w2w_d", tag="ma2", align_bytes=64)
+        deal(w2w_d[:], w2w[:], 2, nc.gpsimd)
+        w2s_d = keep.tile([P, N], U8, name="w2s_d", tag="ma3", align_bytes=64)
+        deal(w2s_d[:], w2s[:], 1, nc.gpsimd)
 
         out_rows = out_0.rearrange("(p t) w -> p t w", t=PACK)
         out_words = out_1[0].rearrange("p n t -> p (n t)").bitcast(I32)

from contextlib import ExitStack

import concourse.mybir as mybir

K, T, S, N, H, G, U = 512, 1024, 512, 512, 512, 2048, 1024
FLOPS = 2 * K * H * S + 2 * K * H * S + 2 * H * N * U

F32 = mybir.dt.float32
BF16 = mybir.dt.bfloat16
I32 = mybir.dt.int32
U32 = mybir.dt.uint32
U16 = mybir.dt.uint16
U8 = mybir.dt.uint8
FP8X4 = mybir.dt.float8_e4m3fn_x4
FP4X4 = mybir.dt.float4_e2m1fn_x4
ALU = mybir.AluOpType
COPY = mybir.ActivationFunctionType.Copy

P = 128
PACK = 4
QUADRANT = 32
BANK = 512
BLOCK = BANK // PACK
STORE = 256
WIDTHS = (128, 256, 256, 256, 128)
STARTS = tuple(sum(WIDTHS[:c]) for c in range(len(WIDTHS)))


def tile_picked_pqkmixpagex_none_po_kernel(
    tc, x_words, x_scales, w1_words, w1_scales, gs, d_words, d_scales, mem, res, gn,
    w2_words, w2_scales, offs, n1, n2, n3, kidx, n4, out_0, out_1, out_2,
):
    nc = tc.nc
    with ExitStack() as ctx:
        keep = ctx.enter_context(tc.tile_pool(name="keep", bufs=1))
        psum = ctx.enter_context(tc.psum_pool(name="psum", bufs=1))

        def load_list(src, name):
            tile = keep.tile([P, S // 16], U16, name=name)
            nc.sync.dma_start(tile[:], src)
            return tile

        def load_words(src, width, name):
            tile = keep.tile([P, width], U32, name=name, align_bytes=64)
            nc.sync.dma_start(tile[:].bitcast(I32), src[0].rearrange("p n t -> p (n t)").bitcast(I32))
            return tile

        def load_fp4(src, name):
            tile = keep.tile([P, 2 * H], U8, name=name, align_bytes=64)
            nc.sync.dma_start(tile[:].bitcast(I32), src[0].bitcast(I32))
            return tile

        def load_scale_rows(src, width, name):
            tile = keep.tile([P, width], U8, name=name, align_bytes=64)
            rows = src[0].bitcast(I32)
            for q in range(P // QUADRANT):
                nc.sync.dma_start(
                    tile[QUADRANT * q : QUADRANT * (q + 1), :].bitcast(I32),
                    rows[4 * q : 4 * q + 4, :].unsqueeze(0).broadcast_to([8, 4, width // 4]),
                )
            return tile

        def load_column(src, name):
            tile = keep.tile([P, PACK], F32, name=name)
            nc.sync.dma_start(tile[:], src.rearrange("(p t) o -> p (t o)", t=PACK))
            return tile

        def deal(dst, src, unit, engine=nc.vector):
            engine.tensor_copy(
                dst.rearrange("p (t m b) -> p t m b", t=PACK, b=unit),
                src.rearrange("p (m t b) -> p t m b", t=PACK, b=unit),
            )

        offs_sb = load_list(offs, "offs_sb")
        xs = load_scale_rows(x_scales, T, "xs")
        w1w = load_fp4(w1_words, "w1w")
        xw = load_words(x_words, T, "xw")
        kidx_sb = load_list(kidx, "kidx_sb")
        w1s = load_scale_rows(w1_scales, H, "w1s")
        ds = keep.tile([P, G], U8, name="ds", align_bytes=64)
        nc.sync.dma_start(
            ds[:].bitcast(I32), d_scales[0].bitcast(I32).unsqueeze(1).broadcast_to([16, 8, G // 4])
        )
        n1_sb = load_list(n1, "n1_sb")
        n2_sb = load_list(n2, "n2_sb")
        n3_sb = load_list(n3, "n3_sb")
        dw = load_words(d_words, G, "dw")
        gs_sb = load_column(gs, "gs_sb")
        page = []
        for t in range(PACK):
            tile = keep.tile([P, U], F32, name=f"page{t}")
            nc.sync.dma_start(tile[:], mem.rearrange("(p t) w -> p t w", t=PACK)[:, t, :])
            page.append(tile)
        n4_sb = load_list(n4, "n4_sb")
        gn_sb = load_column(gn, "gn_sb")
        w2w = load_fp4(w2_words, "w2w")
        w2s = load_scale_rows(w2_scales, N, "w2s")
        res_sb = keep.tile([P, PACK, U], F32, name="res_sb")
        nc.sync.dma_start(res_sb[:], res.rearrange("(p t) w -> p t w", t=PACK))

        zero = keep.tile([P, 1], F32, name="zero")
        nc.vector.memset(zero[:], 0.0)
        ywin = []
        for t in range(PACK):
            tile = keep.tile([P, 2 * S], F32, name=f"ywin{t}")
            nc.scalar.activation(tile[:, S:], zero[:].to_broadcast([P, S]), COPY)
            ywin.append(tile)

        w1w_d = keep.tile([P, 2 * H], U8, name="w1w_d", align_bytes=64)
        deal(w1w_d[:], w1w[:], 2, nc.gpsimd)
        xq_s = keep.tile([P, S], U8, name="xq_s", align_bytes=64)
        nc.vector.tensor_copy(xq_s[:], xs[:].indirect(offs_sb[:]))
        xq_w = keep.tile([P, S], U32, name="xq_w", align_bytes=64)
        nc.vector.tensor_copy(xq_w[:], xw[:].indirect(offs_sb[:]))
        w1s_d = keep.tile([P, H], U8, name="w1s_d", align_bytes=64)
        deal(w1s_d[:], w1s[:], 1, nc.gpsimd)
        for t in range(PACK):
            bank = psum.tile([P, S], F32, name=f"y_bank{t}", tag=f"bank{t}")
            nc.tensor.matmul_mx(
                out=bank[:],
                lhsT=w1w_d[:, 2 * P * t : 2 * P * (t + 1)].bitcast(FP4X4),
                lhsT_scale=w1s_d[:, P * t : P * (t + 1)],
                rhs=xq_w[:].bitcast(FP8X4),
                rhs_scale=xq_s[:],
                start=True,
                stop=True,
            )
            nc.scalar.activation(ywin[t][:, :S], bank[:], COPY)

        dq_s = keep.tile([P, H], U8, name="dq_s", align_bytes=64)
        nc.vector.tensor_copy(dq_s[:], ds[:].indirect(kidx_sb[:]))
        dq_w = keep.tile([P, H], U32, name="dq_w", align_bytes=64)
        dq_s_d = keep.tile([P, H], U8, name="dq_s_d", align_bytes=64)
        dq_w_d = keep.tile([P, H], U32, name="dq_w_d", align_bytes=64)
        key_s = keep.tile([P, H], U8, name="key_s", align_bytes=64)
        nc.gpsimd.memset(key_s[:], 0)

        def place_key_scales():
            deal(dq_s_d[:], dq_s[:], 1)
            for r in range(4):
                nc.sync.dma_start(
                    key_s[r:P:QUADRANT, :].bitcast(I32), dq_s_d[8 * r : P : QUADRANT, :].bitcast(I32)
                )

        def fetch_key_words():
            nc.vector.tensor_copy(dq_w[:], dw[:].indirect(kidx_sb[:]))

        def deal_key_words():
            nc.vector.tensor_copy(
                dq_w_d[:].bitcast(I32).rearrange("p (t m) -> p m t", t=PACK),
                dq_w[:].bitcast(I32).rearrange("p (m t) -> p m t", t=PACK),
            )

        z_bf = keep.tile([P, S, PACK], BF16, name="z_bf", tag="z_bf", align_bytes=64)

        own, top = {}, {}

        def fetch_own(t):
            own[t] = keep.tile([P, S], F32, name=f"ga{t}", tag=f"ga{t}")
            nc.vector.tensor_copy(own[t][:], ywin[t][:].indirect(n1_sb[:]))

        def top_of(t):
            top[t] = keep.tile([P, S], F32, name=f"ma{t}", tag=f"ma{t}", align_bytes=64)
            nc.vector.tensor_tensor(top[t][:], own[t][:], ywin[t][:, :S], ALU.max)

        def fetch_less(t, lst, name):
            tile = keep.tile([P, S], F32, name=f"{name}{t}", tag=f"{name}{t}", align_bytes=64)
            nc.vector.tensor_tensor(tile[:], ywin[t][:].indirect(lst[:]), top[t][:], ALU.subtract)
            return tile

        half_old = []

        def fetch_old(t, tag):
            tile = keep.tile([P, S], F32, name=f"half_old{t}", tag=tag, align_bytes=64)
            nc.vector.tensor_scalar(tile[:], page[t][:].indirect(n4_sb[:]), 0.5, 0.0, ALU.mult, ALU.add)
            half_old.append(tile)

        fetch_own(0)
        place_key_scales()
        top_of(0)
        for t in range(PACK):
            if t + 1 < PACK:
                fetch_own(t + 1)
            e = fetch_less(t, n2_sb, "gb")
            f = fetch_less(t, n3_sb, "gc")
            if t + 1 < PACK:
                top_of(t + 1)
            else:
                fetch_old(0, "ma2")
            diff = keep.tile([P, S], F32, name=f"diff{t}")
            nc.vector.tensor_tensor(diff[:], e[:], f[:], ALU.max)
            nc.scalar.activation(z_bf[:, :, t], diff[:], COPY, scale=gs_sb[:, t : t + 1])
            if t == 0:
                fetch_key_words()
            elif t == 1:
                deal_key_words()
        fetch_old(1, "ma3")
        fetch_old(2, "gb3")

        z_w = keep.tile([P, S], U32, name="z_w", align_bytes=64)
        z_s = keep.tile([P, S], U8, name="z_s", align_bytes=64)
        nc.vector.quantize_mx(
            out=z_w[:].bitcast(FP8X4), scales=z_s[:], in_=z_bf[:].rearrange("p c t -> p (c t)")
        )


        fetch_old(3, "z_bf")

        chunks = range(len(WIDTHS))
        cols = [slice(STARTS[c], STARTS[c] + WIDTHS[c]) for c in chunks]
        z2_bf = keep.tile([P, U * PACK], BF16, name="z2_bf", align_bytes=64)
        z2_planes = z2_bf[:].rearrange("p (c t) -> p c t", t=PACK)
        new = []

        def score(t):
            bank = psum.tile([P, S], F32, name=f"s_bank{t}", tag=f"bank{PACK + t}")
            nc.tensor.matmul_mx(
                out=bank[:],
                lhsT=dq_w_d[:, P * t : P * (t + 1)].bitcast(FP8X4),
                lhsT_scale=key_s[:, P * t : P * (t + 1)],
                rhs=z_w[:].bitcast(FP8X4),
                rhs_scale=z_s[:],
                start=True,
                stop=True,
            )
            tile = keep.tile([P, S], F32, name=f"new{t}")
            nc.vector.scalar_tensor_tensor(tile[:], bank[:], -0.0625, half_old[t][:], ALU.mult, ALU.max)
            new.append(tile)

        def weigh_on_scalar(t, span):
            nc.scalar.activation(z2_planes[:, span, t], page[t][:, span], COPY, scale=gn_sb[:, t : t + 1])

        score(0)
        for t in range(PACK):
            if t + 1 < PACK:
                score(t + 1)
            nc.vector.tensor_copy(page[t][:].indirect(n4_sb[:]), new[t][:])
            if t < 2:
                weigh_on_scalar(t, slice(0, U))
            elif t == 2:
                weigh_on_scalar(t, slice(WIDTHS[0], U))
        for t in (2, 3):
            nc.vector.tensor_scalar(
                z2_planes[:, cols[0], t], page[t][:, cols[0]], gn_sb[:, t : t + 1], None, ALU.mult
            )
        for c in chunks[1:]:
            weigh_on_scalar(3, cols[c])

        w2w_d = keep.tile([P, 2 * N], U8, name="w2w_d", tag="ma2", align_bytes=64)
        deal(w2w_d[:], w2w[:], 2, nc.gpsimd)
        w2s_d = keep.tile([P, N], U8, name="w2s_d", tag="ma3", align_bytes=64)
        deal(w2s_d[:], w2s[:], 1, nc.gpsimd)

        out_rows = out_0.rearrange("(p t) w -> p t w", t=PACK)
        out_words = out_1[0].rearrange("p n t -> p (n t)").bitcast(I32)
        o_w = keep.tile([P, U], U32, name="o_w", align_bytes=64)
        o_s = keep.tile([P, U], U8, name="o_s", align_bytes=64)
        z2_w = keep.tile([P, U], U32, name="z2_w", align_bytes=64)
        z2_s = keep.tile([P, U], U8, name="z2_s", align_bytes=64)
        y_out = [keep.tile([P, PACK, STORE], F32, name=f"y_out{g}") for g in range(U // STORE)]
        o_bf = [keep.tile([P, STORE, PACK], BF16, name=f"o_bf{g}", align_bytes=64) for g in range(U // STORE)]

        def quantise_page(c):
            nc.vector.quantize_mx(
                out=z2_w[:, cols[c]].bitcast(FP8X4),
                scales=z2_s[:, cols[c]],
                in_=z2_bf[:, PACK * STARTS[c] : PACK * (STARTS[c] + WIDTHS[c])],
            )

        def product(b):
            block = slice(BLOCK * b, BLOCK * (b + 1))
            g, part = divmod(BLOCK * b, STORE)
            inside = slice(part, part + BLOCK)
            bank = psum.tile([P, PACK, BLOCK], F32, name=f"o_bank{b}", tag=f"bank{b}")
            for t in range(PACK):
                nc.tensor.matmul_mx(
                    out=bank[:, t, :],
                    lhsT=w2w_d[:, 2 * P * t : 2 * P * (t + 1)].bitcast(FP4X4),
                    lhsT_scale=w2s_d[:, P * t : P * (t + 1)],
                    rhs=z2_w[:, block].bitcast(FP8X4),
                    rhs_scale=z2_s[:, block],
                    start=True,
                    stop=True,
                )
            nc.vector.tensor_tensor(y_out[g][:, :, inside], bank[:], res_sb[:, :, block], ALU.add)
            nc.scalar.activation(
                o_bf[g][:, inside, :].rearrange("p (c i) t -> p c t i", i=4),
                y_out[g][:, :, inside].rearrange("p t (c i) -> p c t i", i=4),
                COPY,
            )
            if part + BLOCK == STORE:
                nc.sync.dma_start(out_rows[:, :, STORE * g : STORE * (g + 1)], y_out[g][:])

        def quantise_out(g):
            span = slice(STORE * g, STORE * (g + 1))
            nc.vector.quantize_mx(
                out=o_w[:, span].bitcast(FP8X4), scales=o_s[:, span], in_=o_bf[g][:].rearrange("p c t -> p (c t)")
            )

        quantise_page(0)
        done = 0
        for c in chunks:
            if c + 1 in chunks:
                quantise_page(c + 1)
            for b in range(done, done + WIDTHS[c] // BLOCK):
                product(b)
            done = done + WIDTHS[c] // BLOCK
        for g in range(U // STORE - 1):
            quantise_out(g)
        nc.sync.dma_start(out_words[:, : U - STORE], o_w[:, : U - STORE].bitcast(I32))
        quantise_out(U // STORE - 1)
        nc.sync.dma_start(out_words[:, U - STORE :], o_w[:, U - STORE :].bitcast(I32))
        out_scales = out_2[0].bitcast(I32)
        for q in range(P // QUADRANT):
            queue = nc.scalar if q % 2 == 0 else nc.sync
            queue.dma_start(
                out_scales[4 * q : 4 * q + 4, :], o_s[QUADRANT * q : QUADRANT * q + 4, :].bitcast(I32)
            )
